import numpy as np, ml_dtypes
CORES = [71,199,327,455]
N = 4
ROOT = 3
def setup_inputs(rng):
    return {"x": rng.standard_normal((N, 128, 256), dtype=np.float32).astype(ml_dtypes.bfloat16)}
def reference(x):
    return {"y": np.broadcast_to(x[ROOT], x.shape)}

@@ -1,0 +1,50 @@
+from concourse.bass import DstId, RemoteDMATransfer
+
+SCRATCH = {
+    "d": ("dram", [2, 128, 128], "bfloat16"),
+}
+SEMAPHORES = ["loaded", "a", "b", "sent", "stored"]
+
+
+def rank_program(g, core, T, topo):
+    rank = T.rank_of(core)
+    if rank is None:
+        return
+    h0, h1, h2, root = T.cores
+    S = T.sem
+    arrive = (S.a, S.b)
+
+    if core == root:
+        def tr(k, dst, mask):
+            rid, pid = topo.addr(dst, core)
+            return RemoteDMATransfer(dst_ids=[DstId(rid=rid, pnc=pid)], dma_engine_mask=mask, remote_sem=arrive[k],
+                                     src=T.d[k], dst=T.d[k])
+        g.dma_start(T.d[:], T.x[:]).then_inc(S.loaded, 16)
+        g.wait_ge(S.loaded, 16)
+        g.remote_dma_fused([tr(0, h2, 0x0F), tr(1, h0, 0xF0)], local_sem=S.sent)
+        g.remote_dma_fused([tr(1, h2, 0x0F), tr(0, h0, 0xF0)], local_sem=S.sent)
+        g.dma_start(T.y[:], T.x[:]).then_inc(S.stored, 16)
+        g.wait_ge(S.sent, 16)
+        g.wait_ge(S.stored, 16)
+        return
+
+    def store(k):
+        g.dma_start(T.y[64 * k:64 * (k + 1), :], T.d[k]).then_inc(S.stored, 16)
+
+    if core == h1:
+        g.wait_ge(S.a, 8)
+        store(0)
+        g.wait_ge(S.b, 8)
+        store(1)
+        g.wait_ge(S.stored, 32)
+        return
+
+    k = 0 if core == h2 else 1
+    rid, pid = topo.addr(h1, core)
+    g.wait_ge(arrive[k], 4)
+    g.remote_dma(T.d[k], T.d[k], remote_sem=arrive[k], local_sem=S.sent, pid=pid, routing_id=rid, dma_engine_mask=0xFF)
+    store(k)
+    g.wait_ge(arrive[1 - k], 4)
+    store(1 - k)
+    g.wait_ge(S.stored, 32)
+    g.wait_ge(S.sent, 8)

@@ -1,9 +1,9 @@
 from concourse.bass import DstId, RemoteDMATransfer
 
 SCRATCH = {
-    "d": ("dram", [2, 128, 128], "bfloat16"),
+    "d": ("dram", [4, 128, 64], "bfloat16"),
 }
-SEMAPHORES = ["loaded", "a", "b", "sent", "stored"]
+SEMAPHORES = ["loaded", "p0", "p1", "r", "a", "b", "sent", "stored"]
 
 
 def rank_program(g, core, T, topo):
@@ -12,39 +12,43 @@ def rank_program(g, core, T, topo):
         return
     h0, h1, h2, root = T.cores
     S = T.sem
-    arrive = (S.a, S.b)
 
     if core == root:
-        def tr(k, dst, mask):
+        def tr(q, dst, mask, sem):
             rid, pid = topo.addr(dst, core)
-            return RemoteDMATransfer(dst_ids=[DstId(rid=rid, pnc=pid)], dma_engine_mask=mask, remote_sem=arrive[k],
-                                     src=T.d[k], dst=T.d[k])
+            return RemoteDMATransfer(dst_ids=[DstId(rid=rid, pnc=pid)], dma_engine_mask=mask, remote_sem=sem,
+                                     src=T.d[q], dst=T.d[q])
         g.dma_start(T.d[:], T.x[:]).then_inc(S.loaded, 16)
         g.wait_ge(S.loaded, 16)
-        g.remote_dma_fused([tr(0, h2, 0x0F), tr(1, h0, 0xF0)], local_sem=S.sent)
-        g.remote_dma_fused([tr(1, h2, 0x0F), tr(0, h0, 0xF0)], local_sem=S.sent)
+        g.remote_dma_fused([tr(0, h2, 0x0F, S.p0), tr(2, h0, 0xF0, S.p0)], local_sem=S.sent)
+        g.remote_dma_fused([tr(1, h2, 0x0F, S.p1), tr(3, h0, 0xF0, S.p1)], local_sem=S.sent)
+        g.remote_dma_fused([tr(2, h2, 0x03, S.r), tr(3, h2, 0x0C, S.r), tr(0, h0, 0x30, S.r), tr(1, h0, 0xC0, S.r)],
+                           local_sem=S.sent)
         g.dma_start(T.y[:], T.x[:]).then_inc(S.stored, 16)
-        g.wait_ge(S.sent, 16)
+        g.wait_ge(S.sent, 24)
         g.wait_ge(S.stored, 16)
         return
 
     def store(k):
-        g.dma_start(T.y[64 * k:64 * (k + 1), :], T.d[k]).then_inc(S.stored, 16)
+        g.dma_start(T.y[64 * k:64 * (k + 1), :], T.d[2 * k:2 * k + 2]).then_inc(S.stored, 16)
 
     if core == h1:
-        g.wait_ge(S.a, 8)
+        g.wait_ge(S.a, 16)
         store(0)
-        g.wait_ge(S.b, 8)
+        g.wait_ge(S.b, 16)
         store(1)
         g.wait_ge(S.stored, 32)
         return
 
     k = 0 if core == h2 else 1
     rid, pid = topo.addr(h1, core)
-    g.wait_ge(arrive[k], 4)
-    g.remote_dma(T.d[k], T.d[k], remote_sem=arrive[k], local_sem=S.sent, pid=pid, routing_id=rid, dma_engine_mask=0xFF)
+    for j, sem in enumerate((S.p0, S.p1)):
+        q = 2 * k + j
+        g.wait_ge(sem, 4)
+        g.remote_dma(T.d[q], T.d[q], remote_sem=(S.a, S.b)[k], local_sem=S.sent, pid=pid, routing_id=rid,
+                     dma_engine_mask=0xFF)
     store(k)
-    g.wait_ge(arrive[1 - k], 4)
+    g.wait_ge(S.r, 4)
     store(1 - k)
     g.wait_ge(S.stored, 32)
-    g.wait_ge(S.sent, 8)
+    g.wait_ge(S.sent, 16)

@@ -3,7 +3,7 @@ from concourse.bass import DstId, RemoteDMATransfer
 SCRATCH = {
     "d": ("dram", [4, 128, 64], "bfloat16"),
 }
-SEMAPHORES = ["loaded", "p0", "p1", "r", "a", "b", "sent", "stored"]
+SEMAPHORES = ["l0", "l1", "p0", "p1", "r", "f0", "f1", "sent", "stored"]
 
 
 def rank_program(g, core, T, topo):
@@ -18,37 +18,33 @@ def rank_program(g, core, T, topo):
             rid, pid = topo.addr(dst, core)
             return RemoteDMATransfer(dst_ids=[DstId(rid=rid, pnc=pid)], dma_engine_mask=mask, remote_sem=sem,
                                      src=T.d[q], dst=T.d[q])
-        g.dma_start(T.d[:], T.x[:]).then_inc(S.loaded, 16)
-        g.wait_ge(S.loaded, 16)
-        g.remote_dma_fused([tr(0, h2, 0x0F, S.p0), tr(2, h0, 0xF0, S.p0)], local_sem=S.sent)
-        g.remote_dma_fused([tr(1, h2, 0x0F, S.p1), tr(3, h0, 0xF0, S.p1)], local_sem=S.sent)
-        g.remote_dma_fused([tr(2, h2, 0x03, S.r), tr(3, h2, 0x0C, S.r), tr(0, h0, 0x30, S.r), tr(1, h0, 0xC0, S.r)],
+        g.dma_start(T.d[0:2], T.x[0:64, :]).then_inc(S.l0, 16)
+        g.dma_start(T.d[2:4], T.x[64:128, :]).then_inc(S.l1, 16)
+        g.wait_ge(S.l0, 16)
+        g.remote_dma_fused([tr(0, h2, 0x0F, S.p0), tr(1, h0, 0xF0, S.p0)], local_sem=S.sent)
+        g.wait_ge(S.l1, 16)
+        g.remote_dma_fused([tr(2, h2, 0x0F, S.p1), tr(3, h0, 0xF0, S.p1)], local_sem=S.sent)
+        g.remote_dma_fused([tr(1, h2, 0x03, S.r), tr(3, h2, 0x0C, S.r), tr(0, h0, 0x30, S.r), tr(2, h0, 0xC0, S.r)],
                            local_sem=S.sent)
         g.dma_start(T.y[:], T.x[:]).then_inc(S.stored, 16)
         g.wait_ge(S.sent, 24)
         g.wait_ge(S.stored, 16)
         return
 
-    def store(k):
-        g.dma_start(T.y[64 * k:64 * (k + 1), :], T.d[2 * k:2 * k + 2]).then_inc(S.stored, 16)
-
     if core == h1:
-        g.wait_ge(S.a, 16)
-        store(0)
-        g.wait_ge(S.b, 16)
-        store(1)
+        for j, sem in enumerate((S.f0, S.f1)):
+            g.wait_ge(sem, 16)
+            g.dma_start(T.y[64 * j:64 * (j + 1), :], T.d[2 * j:2 * j + 2]).then_inc(S.stored, 16)
         g.wait_ge(S.stored, 32)
         return
 
     k = 0 if core == h2 else 1
     rid, pid = topo.addr(h1, core)
-    for j, sem in enumerate((S.p0, S.p1)):
-        q = 2 * k + j
-        g.wait_ge(sem, 4)
-        g.remote_dma(T.d[q], T.d[q], remote_sem=(S.a, S.b)[k], local_sem=S.sent, pid=pid, routing_id=rid,
-                     dma_engine_mask=0xFF)
-    store(k)
+    for j, (got, there) in enumerate(((S.p0, S.f0), (S.p1, S.f1))):
+        q = 2 * j + k
+        g.wait_ge(got, 4)
+        g.remote_dma(T.d[q], T.d[q], remote_sem=there, local_sem=S.sent, pid=pid, routing_id=rid, dma_engine_mask=0xFF)
     g.wait_ge(S.r, 4)
-    store(1 - k)
-    g.wait_ge(S.stored, 32)
+    g.dma_start(T.y[:], T.d[:]).then_inc(S.stored, 16)
+    g.wait_ge(S.stored, 16)
     g.wait_ge(S.sent, 16)

from concourse.bass import DstId, RemoteDMATransfer

SCRATCH = {
    "d": ("dram", [4, 128, 64], "bfloat16"),
}
SEMAPHORES = ["l0", "l1", "p0", "p1", "r", "f0", "f1", "sent", "stored"]


def rank_program(g, core, T, topo):
    rank = T.rank_of(core)
    if rank is None:
        return
    h0, h1, h2, root = T.cores
    S = T.sem

    if core == root:
        def tr(q, dst, mask, sem):
            rid, pid = topo.addr(dst, core)
            return RemoteDMATransfer(dst_ids=[DstId(rid=rid, pnc=pid)], dma_engine_mask=mask, remote_sem=sem,
                                     src=T.d[q], dst=T.d[q])
        g.dma_start(T.d[0:2], T.x[0:64, :]).then_inc(S.l0, 16)
        g.dma_start(T.d[2:4], T.x[64:128, :]).then_inc(S.l1, 16)
        g.wait_ge(S.l0, 16)
        g.remote_dma_fused([tr(0, h2, 0x0F, S.p0), tr(1, h0, 0xF0, S.p0)], local_sem=S.sent)
        g.wait_ge(S.l1, 16)
        g.remote_dma_fused([tr(2, h2, 0x0F, S.p1), tr(3, h0, 0xF0, S.p1)], local_sem=S.sent)
        g.remote_dma_fused([tr(1, h2, 0x03, S.r), tr(3, h2, 0x0C, S.r), tr(0, h0, 0x30, S.r), tr(2, h0, 0xC0, S.r)],
                           local_sem=S.sent)
        g.dma_start(T.y[:], T.x[:]).then_inc(S.stored, 16)
        g.wait_ge(S.sent, 24)
        g.wait_ge(S.stored, 16)
        return

    if core == h1:
        for j, sem in enumerate((S.f0, S.f1)):
            g.wait_ge(sem, 16)
            g.dma_start(T.y[64 * j:64 * (j + 1), :], T.d[2 * j:2 * j + 2]).then_inc(S.stored, 16)
        g.wait_ge(S.stored, 32)
        return

    k = 0 if core == h2 else 1
    rid, pid = topo.addr(h1, core)
    for j, (got, there) in enumerate(((S.p0, S.f0), (S.p1, S.f1))):
        q = 2 * j + k
        g.wait_ge(got, 4)
        g.remote_dma(T.d[q], T.d[q], remote_sem=there, local_sem=S.sent, pid=pid, routing_id=rid, dma_engine_mask=0xFF)
    g.wait_ge(S.r, 4)
    g.dma_start(T.y[:], T.d[:]).then_inc(S.stored, 16)
    g.wait_ge(S.stored, 16)
    g.wait_ge(S.sent, 16)
